import numpy as np
import ml_dtypes


def mxq(x, axis, fmt="e4m3"):
    dtype, down = {"e4m3": (ml_dtypes.float8_e4m3fn, 7), "e5m2": (ml_dtypes.float8_e5m2, 14)}[fmt]
    v = np.moveaxis(np.asarray(x, np.float32).astype(ml_dtypes.bfloat16).astype(np.float64), axis, -1)
    blocks = v.reshape(v.shape[:-1] + (-1, 32))
    amax = np.abs(blocks).max(-1, keepdims=True)
    byte = np.maximum(np.where(amax > 0, np.frexp(amax)[1] - 1 + 127, 0) - down, 1)
    scale = np.exp2(byte - 127.0)
    codes = (blocks / scale).astype(np.float32).astype(dtype).astype(np.float64)
    return np.moveaxis((codes * scale).reshape(v.shape), -1, axis)


WIDE = False


def mx_kscale(k):
    if not WIDE:
        return np.ones(k)
    levels = np.array([10, -10, 5, -5, 0])
    if k % 512:
        return np.exp2(np.random.permutation(np.resize(levels, k // 32))).repeat(32)
    a = np.empty((k // 512, 16))
    for p in range(k // 512):
        a[p, :8] = np.random.permutation(np.resize(levels, 8))
        for g in range(8):
            far = levels[np.abs(levels - a[p, g]) >= 10]
            a[p, g + 8] = far[np.random.randint(len(far))]
    return np.exp2(a.ravel()).repeat(32)


def f64(x):
    return np.asarray(x).astype(np.float64)


def striped(idx):
    return np.tile(idx.reshape(-1, 16).T, (8, 1)).astype(np.uint16)


def unstriped(offs):
    return offs[:16].T.reshape(-1).astype(np.int64)


E2M1 = np.array([0.0, 0.5, 1.0, 1.5, 2.0, 3.0, 4.0, 6.0, -0.0, -0.5, -1.0, -1.5, -2.0, -3.0, -4.0, -6.0])


def pack_weight(w, fmt):
    k, n = w.shape
    w = f64(np.asarray(w, np.float32).astype(ml_dtypes.bfloat16)).reshape(k // 32, 32, n)
    amax = np.abs(w).max(1)
    if fmt == "e4m3":
        byte = np.frexp(amax)[1] - 1 + 127 - 7
    else:
        mant, ex = np.frexp(amax / 6.0)
        byte = np.where(mant > 0.5, ex, ex - 1) + 127
    byte = np.clip(np.where(amax > 0, byte, 1), 1, 254)
    scaled = (w * np.exp2(127.0 - byte)[:, None, :]).reshape(k, n).astype(np.float32)
    by_word = np.ascontiguousarray(scaled.reshape(k // 512, 128, 4, n).transpose(0, 1, 3, 2))
    if fmt == "e4m3":
        words = by_word.astype(ml_dtypes.float8_e4m3fn).view(np.uint8)
    else:
        c = by_word.astype(ml_dtypes.float4_e2m1fn).view(np.uint8) & 0xF
        words = (c[..., 0::2] | (c[..., 1::2] << 4)).reshape(k // 512, 128, 2 * n)
    return np.ascontiguousarray(words), np.ascontiguousarray(byte.astype(np.uint8).reshape(k // 512, 16, n))


def unpack_weight(words, scales, fmt):
    g, _, n = scales.shape
    words = np.ascontiguousarray(words).reshape(g, 128, n, -1)
    if fmt == "e4m3":
        vals = words.view(ml_dtypes.float8_e4m3fn).astype(np.float64)
    else:
        nib = np.empty((g, 128, n, 4), np.uint8)
        nib[..., 0::2] = words & 0xF
        nib[..., 1::2] = words >> 4
        vals = E2M1[nib]
    vals = vals * np.repeat(np.exp2(scales.astype(np.float64) - 127.0), 8, axis=1)[..., None]
    return vals.transpose(0, 1, 3, 2).reshape(g * 512, n)


def gelu(v):
    return 0.5 * v * (1.0 + np.tanh(np.sqrt(2.0 / np.pi) * (v + 0.044715 * v**3)))


K, H, N, T, S, P, P2 = 512, 1536, 768, 4096, 1024, 512, 256

def setup_inputs():
    n = np.random.standard_normal
    s = mx_kscale(K)[:, None]
    u = mx_kscale(H)[:, None]
    tab_words, tab_scales = pack_weight(n((K, T)) * s, "e4m3")
    w1_words, w1_scales = pack_weight(n((K, H)) / s / np.sqrt(K), "e2m1")
    return {
        "tab_words": tab_words,
        "tab_scales": tab_scales,
        "offs": striped(np.random.permutation(T)[:S]),
        "pos1": striped(np.random.permutation(S)[:P]),
        "pos2": striped(np.random.permutation(S)[:P]),
        "pos3": striped(np.random.permutation(P)[:P2]),
        "pos4": striped(np.random.permutation(P)[:P2]),
        "w1_words": w1_words,
        "w1_scales": w1_scales,
        "w2": (n((K, H)) / s / np.sqrt(K)).astype(np.float32),
        "gain": (np.exp(0.3 * n(H)) * u[:, 0]).astype(np.float32),
        "slope": (1.5 * np.exp(0.3 * n(H)) / u[:, 0]).astype(np.float32),
        "w3": (n((H, N)) / u / np.sqrt(H)).astype(np.float32),
    }

def reference(tab_words, tab_scales, offs, pos1, pos2, pos3, pos4, w1_words, w1_scales, w2, gain, slope, w3):
    v = unpack_weight(tab_words, tab_scales, "e4m3")[:, unstriped(offs)]
    w1 = unpack_weight(w1_words, w1_scales, "e2m1")
    d1 = w1.T @ v
    d2 = mxq(f64(w2), 0, "e4m3").T @ v
    h = f64(gain)[:, None] * np.maximum(d1, d2)
    litter = h[:, unstriped(pos1)]
    canopy = h[:, unstriped(pos2)]
    x = litter * np.tanh(f64(slope)[:, None] * canopy)
    y = mxq(f64(w3), 0, "e4m3").T @ mxq(x, 0, "e4m3")
    return np.abs(y[:, unstriped(pos3)] - y[:, unstriped(pos4)])

@@ -1,0 +1,298 @@
+from contextlib import ExitStack
+
+import concourse.mybir as mybir
+
+K, H, N, T, S, PM, PJ = 512, 1536, 768, 4096, 1024, 512, 256
+FLOPS = 2 * (2 * K * H * S + H * N * PM)
+
+F32 = mybir.dt.float32
+BF16 = mybir.dt.bfloat16
+I32 = mybir.dt.int32
+U32 = mybir.dt.uint32
+U16 = mybir.dt.uint16
+U8 = mybir.dt.uint8
+FP8X4 = mybir.dt.float8_e4m3fn_x4
+FP4X4 = mybir.dt.float4_e2m1fn_x4
+ALU = mybir.AluOpType
+ACT = mybir.ActivationFunctionType
+
+P = 128
+PACK = 4
+PASS = P * PACK
+BANK = 512
+PASSES = H // PASS
+SLICES = H // P
+HALVES = S // BANK
+NSLICES = N // P
+W3_PIECE = 128
+W3_QUANT = 384
+
+
+def tile_list_litter_canopy_contrast_kernel(
+    tc, tab_words, tab_scales, offs, pos1, pos2, pos3, pos4, w1_words, w1_scales, w2, gain, slope, w3, out
+):
+    nc = tc.nc
+    with ExitStack() as ctx:
+        keep = ctx.enter_context(tc.tile_pool(name="keep", bufs=1))
+        stage = ctx.enter_context(tc.tile_pool(name="stage", bufs=1))
+        ring2 = ctx.enter_context(tc.tile_pool(name="ring2", bufs=2))
+        ring3 = ctx.enter_context(tc.tile_pool(name="ring3", bufs=3))
+        ring4 = ctx.enter_context(tc.tile_pool(name="ring4", bufs=4))
+        psum = ctx.enter_context(tc.psum_pool(name="psum", bufs=2))
+        psum_y = ctx.enter_context(tc.psum_pool(name="psum_y", bufs=4))
+
+        def load_list(src, name):
+            t = keep.tile(list(src.shape), U16, name=name)
+            nc.sync.dma_start(t[:], src)
+            return t
+
+        def load_scale_rows(queues, plane, src):
+            for q, queue in enumerate(queues):
+                queue.dma_start(plane[32 * q : 32 * q + 4, :], src[0, 4 * q : 4 * q + 4, :].bitcast(I32))
+
+        tab_s = keep.tile([P, T // 4], I32, name="tab_s", align_bytes=64)
+        nc.vector.memset(tab_s[:], 0)
+        w1_s_raw = keep.tile([P, H // 4], I32, name="w1_s_raw", align_bytes=64)
+        nc.gpsimd.memset(w1_s_raw[:], 0)
+
+        def load_w2(b):
+            raw = stage.tile([P, PACK, PASS], F32, name="w2_raw", tag="ab"[b % 2])
+            nc.sync.dma_start(raw[:], w2[:, PASS * b : PASS * (b + 1)].rearrange("(p j) c -> p j c", j=PACK))
+            return raw
+
+        def load_w3(b):
+            raw = stage.tile([P, PACK, N], F32, name="w3_raw", tag="ba"[b % 2])
+            nc.sync.dma_start(raw[:], w3[PASS * b : PASS * (b + 1), :].rearrange("(p j) n -> p j n", j=PACK))
+            return raw
+
+        w2_raw = {0: load_w2(0)}
+        offs_t = load_list(offs, "offs_t")
+        pos2_t = load_list(pos2, "pos2_t")
+        pos1_t = load_list(pos1, "pos1_t")
+        pos3_t = load_list(pos3, "pos3_t")
+        pos4_t = load_list(pos4, "pos4_t")
+        gain_t = keep.tile([P, PASSES, PACK], F32, name="gain_t")
+        nc.sync.dma_start(gain_t[:], gain.rearrange("(b p t) -> p b t", p=P, t=PACK))
+        tab_w = keep.tile([P, T], I32, name="tab_w", align_bytes=64)
+        nc.sync.dma_start(tab_w[:], tab_words[0].rearrange("p t i -> p (t i)").bitcast(I32))
+        w1_w_raw = stage.tile([P, H // 2], I32, name="w1_w_raw", tag="b")
+        nc.sync.dma_start(w1_w_raw[:], w1_words[0].bitcast(I32))
+        load_scale_rows([nc.scalar] * 4, tab_s, tab_scales)
+        load_scale_rows([nc.scalar, nc.scalar, nc.gpsimd, nc.gpsimd], w1_s_raw, w1_scales)
+        slope_t = keep.tile([P, PASSES, PACK], F32, name="slope_t")
+        nc.gpsimd.dma_start(slope_t[:], slope.rearrange("(b p t) -> p b t", p=P, t=PACK))
+
+        gabs = keep.tile([P, PASSES * PACK], F32, name="gabs")
+        gflat = gain_t[:].rearrange("p b t -> p (b t)")
+        nc.vector.scalar_tensor_tensor(gabs[:], gflat, -1.0, gflat, ALU.mult, ALU.max)
+        slope_f = slope_t[:].rearrange("p b t -> p (b t)")
+
+        w1_s = keep.tile([P, H], U8, name="w1_s", align_bytes=64)
+        nc.vector.tensor_copy(
+            w1_s[:].rearrange("p (b t m) -> p b t m", b=PASSES, t=PACK),
+            w1_s_raw[:].bitcast(U8).rearrange("p (b m t) -> p b t m", b=PASSES, t=PACK),
+        )
+        w1_w = {}
+
+        def deal_w1(b):
+            w1_w[b] = keep.tile([P, PASS], U16, name="w1_w%d" % b, align_bytes=64)
+            nc.vector.tensor_copy(
+                w1_w[b][:].rearrange("p (t m) -> p t m", t=PACK),
+                w1_w_raw[:].bitcast(U16)[:, PASS * b : PASS * (b + 1)].rearrange("p (m t) -> p t m", t=PACK),
+            )
+
+        w2_q = {}
+
+        def cast_w2(b):
+            grouped = ring2.tile([P, PASS * PACK], BF16, name="w2_bf", align_bytes=64)
+            for u in range(4):
+                ms = slice(32 * u, 32 * (u + 1))
+                nc.scalar.copy(
+                    grouped[:].rearrange("p (t m j) -> p m j t", t=PACK, j=PACK)[:, ms],
+                    w2_raw[b][:].rearrange("p j (m t) -> p m j t", t=PACK)[:, ms],
+                )
+            return grouped
+
+        def quantize(grouped, width, name):
+            codes = keep.tile([P, width], U32, name=name + "_c", align_bytes=64)
+            scales = keep.tile([P, width], U8, name=name + "_s", align_bytes=64)
+            nc.vector.quantize_mx(out=codes[:].bitcast(FP8X4), scales=scales[:], in_=grouped[:])
+            return codes, scales
+
+        def interleave(dst, src, copy=nc.scalar.copy):
+            copy(
+                dst.rearrange("p (c i t) -> p c t i", i=4, t=PACK),
+                src.rearrange("p t (c i) -> p c t i", i=4),
+            )
+
+        w2_q[0] = quantize(cast_w2(0), PASS, "w2q0")
+        w2_raw[2] = load_w2(2)
+
+        v_s = keep.tile([P, S], U8, name="v_s", align_bytes=64)
+        nc.vector.tensor_copy(v_s[:], tab_s[:].bitcast(U8).indirect(offs_t[:]))
+        v_w = []
+        for hf in range(HALVES):
+            t = keep.tile([P, BANK], U32, name="v_w%d" % hf, align_bytes=64)
+            cols = BANK // 16
+            nc.vector.tensor_copy(t[:], tab_w[:].bitcast(U32).indirect(offs_t[:, hf * cols : (hf + 1) * cols]))
+            v_w.append(t)
+            if hf == 0:
+                deal_w1(0)
+        deal_w1(1)
+        deal_w1(2)
+        w2_raw[1] = load_w2(1)
+
+        w3_raw = {}
+        w3_q = {}
+        w3_bf = {}
+        h_t = {}
+        bent = {}
+        x4 = {}
+        x_q = {}
+
+        def first_stage(s, hf):
+            b, t = divmod(s, PACK)
+            tok = slice(hf * BANK, (hf + 1) * BANK)
+            rows = slice(s * P, (s + 1) * P)
+            d1 = psum.tile([P, BANK], F32, name="d1")
+            nc.tensor.matmul_mx(
+                out=d1[:],
+                lhsT=w1_w[b][:, t * P : (t + 1) * P].bitcast(FP4X4),
+                lhsT_scale=w1_s[:, rows],
+                rhs=v_w[hf][:].bitcast(FP8X4),
+                rhs_scale=v_s[:, tok],
+                start=True,
+                stop=True,
+            )
+            d2 = psum.tile([P, BANK], F32, name="d2")
+            codes, scales = w2_q[b]
+            nc.tensor.matmul_mx(
+                out=d2[:],
+                lhsT=codes[:, t * P : (t + 1) * P].bitcast(FP8X4),
+                lhsT_scale=scales[:, t * P : (t + 1) * P],
+                rhs=v_w[hf][:].bitcast(FP8X4),
+                rhs_scale=v_s[:, tok],
+                start=True,
+                stop=True,
+            )
+            a = ring4.tile([P, BANK], F32, name="a")
+            nc.scalar.activation(a[:], d1[:], ACT.Copy, scale=gabs[:, s : s + 1])
+            if hf == 0:
+                h_t[s] = ring4.tile([P, S], F32, name="h")
+            nc.vector.scalar_tensor_tensor(h_t[s][:, tok], d2[:], gabs[:, s : s + 1], a[:], ALU.mult, ALU.max)
+
+        def canopy(s):
+            c = ring2.tile([P, PM], F32, name="c")
+            nc.vector.tensor_copy(c[:], h_t[s][:].indirect(pos2_t[:]))
+            bent[s] = ring3.tile([P, PM], F32, name="bent")
+            nc.scalar.activation(bent[s][:], c[:], ACT.Tanh, scale=slope_f[:, s : s + 1])
+
+        def litter(s, lo=0, hi=PM):
+            b, t = divmod(s, PACK)
+            if t == 0:
+                x4[b] = ring2.tile([P, PACK, PM], F32, name="x4")
+            nc.vector.tensor_tensor(
+                x4[b][:, t, lo:hi], h_t[s][:].indirect(pos1_t[:, lo // 16 : hi // 16]), bent[s][:, lo:hi], ALU.mult
+            )
+
+        def round_x(b):
+            xb = ring2.tile([P, PM * PACK], BF16, name="xb", align_bytes=64)
+            for u in range(4):
+                interleave(xb[:, u * 512 : (u + 1) * 512], x4[b][:, :, u * P : (u + 1) * P])
+            return xb
+
+        def cast_w3(piece):
+            b, r = divmod(piece, N // W3_PIECE)
+            u, o = divmod(r * W3_PIECE, W3_QUANT)
+            if o == 0:
+                w3_bf[b, u] = ring2.tile([P, W3_QUANT * PACK], BF16, name="w3_bf", align_bytes=64)
+            interleave(
+                w3_bf[b, u][:, o * PACK : (o + W3_PIECE) * PACK],
+                w3_raw[b][:, :, r * W3_PIECE : (r + 1) * W3_PIECE],
+            )
+            if o + W3_PIECE == W3_QUANT:
+                w3_q[b, u] = quantize(w3_bf[b, u], W3_QUANT, "w3q%d_%d" % (b, u))
+
+        y_ps = {}
+
+        def second_stage(n, b, xq, cols, stop):
+            if b == 0:
+                if n < 4:
+                    y_ps[n] = psum_y.tile([P, PM], F32, name="y")
+                else:
+                    y_ps[n] = psum.tile([P, PM], F32, name="d1" if n == 4 else "d2")
+            u, o = divmod(n * P, W3_QUANT)
+            codes, scales = w3_q[b, u]
+            nc.tensor.matmul_mx(
+                out=y_ps[n][:, cols],
+                lhsT=codes[:, o : o + P].bitcast(FP8X4),
+                lhsT_scale=scales[:, o : o + P],
+                rhs=xq[0][:].bitcast(FP8X4),
+                rhs_scale=xq[1][:],
+                start=(b == 0),
+                stop=stop,
+            )
+
+        xb = {}
+        for s in range(SLICES + 1):
+            if s == 1:
+                w2_q[1] = quantize(cast_w2(1), PASS, "w2q1")
+                w3_raw[0] = load_w3(0)
+            if s == 3:
+                w2_q[2] = quantize(cast_w2(2), PASS, "w2q2")
+                w3_raw[1] = load_w3(1)
+            if s < SLICES:
+                first_stage(s, 0)
+            if 1 <= s <= SLICES:
+                canopy(s - 1)
+            if s < SLICES:
+                first_stage(s, 1)
+            if s >= 2:
+                litter(s - 2)
+                if (s - 2) % PACK == PACK - 1:
+                    xb[(s - 2) // PACK] = round_x((s - 2) // PACK)
+            if s >= 3 and (s - 3) % PACK == PACK - 1:
+                b = (s - 3) // PACK
+                x_q[b] = quantize(xb[b], PM, "xq%d" % b)
+            if 4 <= s < 13:
+                if s == 7:
+                    w3_raw[2] = load_w3(2)
+                cast_w3(2 * (s - 4))
+                cast_w3(2 * (s - 4) + 1)
+            if s == SLICES - 1:
+                for b in range(PASSES - 1):
+                    for n in range(4):
+                        second_stage(n, b, x_q[b], slice(0, PM), False)
+            if s == SLICES:
+                for b in range(PASSES - 1):
+                    for n in range(4, NSLICES):
+                        second_stage(n, b, x_q[b], slice(0, PM), False)
+        last = PASSES - 1
+        HM = PM // 2
+        litter(SLICES - 1, 0, HM)
+        xa = keep.tile([P, HM * PACK], BF16, name="xa", align_bytes=64)
+        for u in range(2):
+            interleave(xa[:, u * 512 : (u + 1) * 512], x4[last][:, :, u * P : (u + 1) * P])
+        litter(SLICES - 1, HM, PM)
+        xz = keep.tile([P, HM * PACK], BF16, name="xz", align_bytes=64)
+        interleave(xz[:], x4[last][:, :, HM:PM], nc.vector.tensor_copy)
+        qa = quantize(xa, HM, "xqa")
+        qz = quantize(xz, HM, "xqz")
+        for n in range(NSLICES):
+            second_stage(n, last, qa, slice(0, HM), False)
+            second_stage(n, last, qz, slice(HM, PM), True)
+
+        y_sb = {}
+        near = {}
+        for n in range(NSLICES + 1):
+            if n < NSLICES:
+                y_sb[n] = ring3.tile([P, PM], F32, name="y_sb")
+                nc.scalar.copy(y_sb[n][:], y_ps[n][:])
+                near[n] = ring3.tile([P, PJ], F32, name="near")
+                nc.vector.tensor_copy(near[n][:], y_sb[n][:].indirect(pos3_t[:]))
+            if n >= 1:
+                diff = ring2.tile([P, PJ], F32, name="diff")
+                nc.vector.tensor_tensor(diff[:], y_sb[n - 1][:].indirect(pos4_t[:]), near[n - 1][:], ALU.subtract)
+                res = ring3.tile([P, PJ], F32, name="res")
+                nc.scalar.activation(res[:], diff[:], ACT.Abs)
+                nc.sync.dma_start(out[(n - 1) * P : n * P, :], res[:])

@@ -24,8 +24,9 @@ PASSES = H // PASS
 SLICES = H // P
 HALVES = S // BANK
 NSLICES = N // P
-W3_PIECE = 128
+PIECE = 128
 W3_QUANT = 384
+PIECES_A_STEP = 3
 
 
 def tile_list_litter_canopy_contrast_kernel(
@@ -34,7 +35,6 @@ def tile_list_litter_canopy_contrast_kernel(
     nc = tc.nc
     with ExitStack() as ctx:
         keep = ctx.enter_context(tc.tile_pool(name="keep", bufs=1))
-        stage = ctx.enter_context(tc.tile_pool(name="stage", bufs=1))
         ring2 = ctx.enter_context(tc.tile_pool(name="ring2", bufs=2))
         ring3 = ctx.enter_context(tc.tile_pool(name="ring3", bufs=3))
         ring4 = ctx.enter_context(tc.tile_pool(name="ring4", bufs=4))
@@ -50,68 +50,54 @@ def tile_list_litter_canopy_contrast_kernel(
             for q, queue in enumerate(queues):
                 queue.dma_start(plane[32 * q : 32 * q + 4, :], src[0, 4 * q : 4 * q + 4, :].bitcast(I32))
 
-        tab_s = keep.tile([P, T // 4], I32, name="tab_s", align_bytes=64)
-        nc.vector.memset(tab_s[:], 0)
-        w1_s_raw = keep.tile([P, H // 4], I32, name="w1_s_raw", align_bytes=64)
-        nc.gpsimd.memset(w1_s_raw[:], 0)
-
-        def load_w2(b):
-            raw = stage.tile([P, PACK, PASS], F32, name="w2_raw", tag="ab"[b % 2])
+        def load_w2(b, tag):
+            raw = keep.tile([P, PACK, PASS], F32, name="w2_raw", tag=tag)
             nc.sync.dma_start(raw[:], w2[:, PASS * b : PASS * (b + 1)].rearrange("(p j) c -> p j c", j=PACK))
             return raw
 
-        def load_w3(b):
-            raw = stage.tile([P, PACK, N], F32, name="w3_raw", tag="ba"[b % 2])
+        def load_w3(b, tag):
+            raw = keep.tile([P, PACK, N], F32, name="w3_raw", tag=tag)
             nc.sync.dma_start(raw[:], w3[PASS * b : PASS * (b + 1), :].rearrange("(p j) n -> p j n", j=PACK))
             return raw
 
-        w2_raw = {0: load_w2(0)}
+        tab_s = keep.tile([P, T // 4], I32, name="tab_s", tag="stage_b")
+        nc.vector.memset(tab_s[:], 0)
+        w1_s_raw = keep.tile([P, H // 4], I32, name="w1_s_raw")
+        nc.gpsimd.memset(w1_s_raw[:], 0)
+
         offs_t = load_list(offs, "offs_t")
         pos2_t = load_list(pos2, "pos2_t")
         pos1_t = load_list(pos1, "pos1_t")
         pos3_t = load_list(pos3, "pos3_t")
         pos4_t = load_list(pos4, "pos4_t")
-        gain_t = keep.tile([P, PASSES, PACK], F32, name="gain_t")
-        nc.sync.dma_start(gain_t[:], gain.rearrange("(b p t) -> p b t", p=P, t=PACK))
-        tab_w = keep.tile([P, T], I32, name="tab_w", align_bytes=64)
-        nc.sync.dma_start(tab_w[:], tab_words[0].rearrange("p t i -> p (t i)").bitcast(I32))
-        w1_w_raw = stage.tile([P, H // 2], I32, name="w1_w_raw", tag="b")
+        w2_raw = {0: load_w2(0, "stage_a")}
+        w1_w_raw = keep.tile([P, H // 2], I32, name="w1_w_raw")
         nc.sync.dma_start(w1_w_raw[:], w1_words[0].bitcast(I32))
+        tab_w = keep.tile([P, T], I32, name="tab_w", tag="stage_c")
+        nc.sync.dma_start(tab_w[:], tab_words[0].rearrange("p t i -> p (t i)").bitcast(I32))
         load_scale_rows([nc.scalar] * 4, tab_s, tab_scales)
         load_scale_rows([nc.scalar, nc.scalar, nc.gpsimd, nc.gpsimd], w1_s_raw, w1_scales)
+        gain_t = keep.tile([P, PASSES, PACK], F32, name="gain_t")
+        nc.gpsimd.dma_start(gain_t[:], gain.rearrange("(b p t) -> p b t", p=P, t=PACK))
         slope_t = keep.tile([P, PASSES, PACK], F32, name="slope_t")
         nc.gpsimd.dma_start(slope_t[:], slope.rearrange("(b p t) -> p b t", p=P, t=PACK))
-
-        gabs = keep.tile([P, PASSES * PACK], F32, name="gabs")
-        gflat = gain_t[:].rearrange("p b t -> p (b t)")
-        nc.vector.scalar_tensor_tensor(gabs[:], gflat, -1.0, gflat, ALU.mult, ALU.max)
         slope_f = slope_t[:].rearrange("p b t -> p (b t)")
 
+        w1_w = keep.tile([P, H], U16, name="w1_w", align_bytes=64)
+        nc.vector.tensor_copy(
+            w1_w[:].rearrange("p (b t m) -> p b t m", b=PASSES, t=PACK),
+            w1_w_raw[:].bitcast(U16).rearrange("p (b m t) -> p b t m", b=PASSES, t=PACK),
+        )
+        v_s = keep.tile([P, S], U8, name="v_s", align_bytes=64)
+        nc.vector.tensor_copy(v_s[:], tab_s[:].bitcast(U8).indirect(offs_t[:]))
         w1_s = keep.tile([P, H], U8, name="w1_s", align_bytes=64)
         nc.vector.tensor_copy(
             w1_s[:].rearrange("p (b t m) -> p b t m", b=PASSES, t=PACK),
             w1_s_raw[:].bitcast(U8).rearrange("p (b m t) -> p b t m", b=PASSES, t=PACK),
         )
-        w1_w = {}
-
-        def deal_w1(b):
-            w1_w[b] = keep.tile([P, PASS], U16, name="w1_w%d" % b, align_bytes=64)
-            nc.vector.tensor_copy(
-                w1_w[b][:].rearrange("p (t m) -> p t m", t=PACK),
-                w1_w_raw[:].bitcast(U16)[:, PASS * b : PASS * (b + 1)].rearrange("p (m t) -> p t m", t=PACK),
-            )
-
-        w2_q = {}
-
-        def cast_w2(b):
-            grouped = ring2.tile([P, PASS * PACK], BF16, name="w2_bf", align_bytes=64)
-            for u in range(4):
-                ms = slice(32 * u, 32 * (u + 1))
-                nc.scalar.copy(
-                    grouped[:].rearrange("p (t m j) -> p m j t", t=PACK, j=PACK)[:, ms],
-                    w2_raw[b][:].rearrange("p j (m t) -> p m j t", t=PACK)[:, ms],
-                )
-            return grouped
+        gabs = keep.tile([P, SLICES], F32, name="gabs")
+        gflat = gain_t[:].rearrange("p b t -> p (b t)")
+        nc.vector.scalar_tensor_tensor(gabs[:], gflat, -1.0, gflat, ALU.mult, ALU.max)
 
         def quantize(grouped, width, name):
             codes = keep.tile([P, width], U32, name=name + "_c", align_bytes=64)
@@ -125,30 +111,53 @@ def tile_list_litter_canopy_contrast_kernel(
                 src.rearrange("p t (c i) -> p c t i", i=4),
             )
 
-        w2_q[0] = quantize(cast_w2(0), PASS, "w2q0")
-        w2_raw[2] = load_w2(2)
+        w2_bf, w2_q = {}, {}
+        w3_raw, w3_bf, w3_q = {}, {}, {}
+        h_t, c_t, bent, x4, x_bf, x_q = {}, {}, {}, {}, {}, {}
 
-        v_s = keep.tile([P, S], U8, name="v_s", align_bytes=64)
-        nc.vector.tensor_copy(v_s[:], tab_s[:].bitcast(U8).indirect(offs_t[:]))
+        def round_w2(b, u):
+            if u == 0:
+                w2_bf[b] = ring2.tile([P, PASS * PACK], BF16, name="w2_bf", align_bytes=64)
+            ms = slice(32 * u, 32 * (u + 1))
+            nc.scalar.copy(
+                w2_bf[b][:].rearrange("p (t m j) -> p m j t", t=PACK, j=PACK)[:, ms],
+                w2_raw[b][:].rearrange("p j (m t) -> p m j t", t=PACK)[:, ms],
+            )
+            if u == 3:
+                w2_q[b] = quantize(w2_bf[b], PASS, "w2q%d" % b)
+                if b == 0:
+                    w2_raw[1] = load_w2(1, "stage_a")
+                else:
+                    w3_raw[b] = load_w3(b, "stage_a" if b == 1 else "stage_b")
+
+        def round_w3(b, r):
+            u, o = divmod(r * PIECE, W3_QUANT)
+            if o == 0:
+                w3_bf[b, u] = ring2.tile([P, W3_QUANT * PACK], BF16, name="w3_bf", align_bytes=64)
+            interleave(w3_bf[b, u][:, o * PACK : (o + PIECE) * PACK], w3_raw[b][:, :, r * PIECE : (r + 1) * PIECE])
+            if o + PIECE == W3_QUANT:
+                w3_q[b, u] = quantize(w3_bf[b, u], W3_QUANT, "w3q%d_%d" % (b, u))
+
+        def round_x(b, u):
+            if u == 0:
+                x_bf[b] = ring2.tile([P, PM * PACK], BF16, name="x_bf", align_bytes=64)
+            interleave(x_bf[b][:, u * PIECE * PACK : (u + 1) * PIECE * PACK], x4[b][:, :, u * PIECE : (u + 1) * PIECE])
+            if u == 3:
+                x_q[b] = quantize(x_bf[b], PM, "xq%d" % b)
+                for n in range(4):
+                    second_stage(n, b, x_q[b], slice(0, PM), False)
+
+        for u in range(4):
+            round_w2(0, u)
+        w2_raw[2] = load_w2(2, "stage_b")
+
         v_w = []
         for hf in range(HALVES):
             t = keep.tile([P, BANK], U32, name="v_w%d" % hf, align_bytes=64)
             cols = BANK // 16
             nc.vector.tensor_copy(t[:], tab_w[:].bitcast(U32).indirect(offs_t[:, hf * cols : (hf + 1) * cols]))
             v_w.append(t)
-            if hf == 0:
-                deal_w1(0)
-        deal_w1(1)
-        deal_w1(2)
-        w2_raw[1] = load_w2(1)
-
-        w3_raw = {}
-        w3_q = {}
-        w3_bf = {}
-        h_t = {}
-        bent = {}
-        x4 = {}
-        x_q = {}
+        w3_raw[0] = load_w3(0, "stage_c")
 
         def first_stage(s, hf):
             b, t = divmod(s, PACK)
@@ -157,7 +166,7 @@ def tile_list_litter_canopy_contrast_kernel(
             d1 = psum.tile([P, BANK], F32, name="d1")
             nc.tensor.matmul_mx(
                 out=d1[:],
-                lhsT=w1_w[b][:, t * P : (t + 1) * P].bitcast(FP4X4),
+                lhsT=w1_w[:, rows].bitcast(FP4X4),
                 lhsT_scale=w1_s[:, rows],
                 rhs=v_w[hf][:].bitcast(FP8X4),
                 rhs_scale=v_s[:, tok],
@@ -182,10 +191,12 @@ def tile_list_litter_canopy_contrast_kernel(
             nc.vector.scalar_tensor_tensor(h_t[s][:, tok], d2[:], gabs[:, s : s + 1], a[:], ALU.mult, ALU.max)
 
         def canopy(s):
-            c = ring2.tile([P, PM], F32, name="c")
-            nc.vector.tensor_copy(c[:], h_t[s][:].indirect(pos2_t[:]))
-            bent[s] = ring3.tile([P, PM], F32, name="bent")
-            nc.scalar.activation(bent[s][:], c[:], ACT.Tanh, scale=slope_f[:, s : s + 1])
+            c_t[s] = keep.tile([P, PM], F32, name="c")
+            nc.vector.tensor_copy(c_t[s][:], h_t[s][:].indirect(pos2_t[:]))
+
+        def bend(s):
+            bent[s] = ring2.tile([P, PM], F32, name="bent")
+            nc.scalar.activation(bent[s][:], c_t[s][:], ACT.Tanh, scale=slope_f[:, s : s + 1])
 
         def litter(s, lo=0, hi=PM):
             b, t = divmod(s, PACK)
@@ -194,24 +205,6 @@ def tile_list_litter_canopy_contrast_kernel(
             nc.vector.tensor_tensor(
                 x4[b][:, t, lo:hi], h_t[s][:].indirect(pos1_t[:, lo // 16 : hi // 16]), bent[s][:, lo:hi], ALU.mult
             )
-
-        def round_x(b):
-            xb = ring2.tile([P, PM * PACK], BF16, name="xb", align_bytes=64)
-            for u in range(4):
-                interleave(xb[:, u * 512 : (u + 1) * 512], x4[b][:, :, u * P : (u + 1) * P])
-            return xb
-
-        def cast_w3(piece):
-            b, r = divmod(piece, N // W3_PIECE)
-            u, o = divmod(r * W3_PIECE, W3_QUANT)
-            if o == 0:
-                w3_bf[b, u] = ring2.tile([P, W3_QUANT * PACK], BF16, name="w3_bf", align_bytes=64)
-            interleave(
-                w3_bf[b, u][:, o * PACK : (o + W3_PIECE) * PACK],
-                w3_raw[b][:, :, r * W3_PIECE : (r + 1) * W3_PIECE],
-            )
-            if o + W3_PIECE == W3_QUANT:
-                w3_q[b, u] = quantize(w3_bf[b, u], W3_QUANT, "w3q%d_%d" % (b, u))
 
         y_ps = {}
 
@@ -233,42 +226,35 @@ def tile_list_litter_canopy_contrast_kernel(
                 stop=stop,
             )
 
-        xb = {}
+        jobs = [(round_w2, b, u) for b in range(1, PASSES) for u in range(4)]
+        jobs = jobs + [(round_w3, b, r) for b in range(PASSES) for r in range(NSLICES)]
         for s in range(SLICES + 1):
-            if s == 1:
-                w2_q[1] = quantize(cast_w2(1), PASS, "w2q1")
-                w3_raw[0] = load_w3(0)
-            if s == 3:
-                w2_q[2] = quantize(cast_w2(2), PASS, "w2q2")
-                w3_raw[1] = load_w3(1)
             if s < SLICES:
                 first_stage(s, 0)
-            if 1 <= s <= SLICES:
+            if s >= 2:
+                bend(s - 2)
+            if s >= 1:
                 canopy(s - 1)
             if s < SLICES:
                 first_stage(s, 1)
+            if s >= 1:
+                count = PIECES_A_STEP - 1 if s in (9, 11) else PIECES_A_STEP
+                for fn, b, u in jobs[:count]:
+                    fn(b, u)
+                jobs = jobs[count:]
             if s >= 2:
                 litter(s - 2)
                 if (s - 2) % PACK == PACK - 1:
-                    xb[(s - 2) // PACK] = round_x((s - 2) // PACK)
-            if s >= 3 and (s - 3) % PACK == PACK - 1:
-                b = (s - 3) // PACK
-                x_q[b] = quantize(xb[b], PM, "xq%d" % b)
-            if 4 <= s < 13:
-                if s == 7:
-                    w3_raw[2] = load_w3(2)
-                cast_w3(2 * (s - 4))
-                cast_w3(2 * (s - 4) + 1)
+                    jobs = [(round_x, (s - 2) // PACK, u) for u in range(4)] + jobs
             if s == SLICES - 1:
-                for b in range(PASSES - 1):
-                    for n in range(4):
-                        second_stage(n, b, x_q[b], slice(0, PM), False)
-            if s == SLICES:
                 for b in range(PASSES - 1):
                     for n in range(4, NSLICES):
                         second_stage(n, b, x_q[b], slice(0, PM), False)
+        assert not jobs
+
         last = PASSES - 1
         HM = PM // 2
+        bend(SLICES - 1)
         litter(SLICES - 1, 0, HM)
         xa = keep.tile([P, HM * PACK], BF16, name="xa", align_bytes=64)
         for u in range(2):
@@ -282,17 +268,18 @@ def tile_list_litter_canopy_contrast_kernel(
             second_stage(n, last, qa, slice(0, HM), False)
             second_stage(n, last, qz, slice(HM, PM), True)
 
+        freed = ["w3q2_0_c", "w3q2_1_c", "xqa_c", "xqz_c", "diff4", "diff5"]
         y_sb = {}
         near = {}
         for n in range(NSLICES + 1):
             if n < NSLICES:
-                y_sb[n] = ring3.tile([P, PM], F32, name="y_sb")
+                y_sb[n] = keep.tile([P, PM], F32, name="y_sb%d" % n)
                 nc.scalar.copy(y_sb[n][:], y_ps[n][:])
-                near[n] = ring3.tile([P, PJ], F32, name="near")
+                near[n] = keep.tile([P, PJ], F32, name="near%d" % n)
                 nc.vector.tensor_copy(near[n][:], y_sb[n][:].indirect(pos3_t[:]))
             if n >= 1:
-                diff = ring2.tile([P, PJ], F32, name="diff")
+                diff = keep.tile([P, PJ], F32, name="diff", tag=freed[n - 1], align_bytes=64)
                 nc.vector.tensor_tensor(diff[:], y_sb[n - 1][:].indirect(pos4_t[:]), near[n - 1][:], ALU.subtract)
-                res = ring3.tile([P, PJ], F32, name="res")
+                res = keep.tile([P, PJ], F32, name="res%d" % n)
                 nc.scalar.activation(res[:], diff[:], ACT.Abs)
                 nc.sync.dma_start(out[(n - 1) * P : n * P, :], res[:])

@@ -46,9 +46,9 @@ def tile_list_litter_canopy_contrast_kernel(
             nc.sync.dma_start(t[:], src)
             return t
 
-        def load_scale_rows(queues, plane, src):
-            for q, queue in enumerate(queues):
-                queue.dma_start(plane[32 * q : 32 * q + 4, :], src[0, 4 * q : 4 * q + 4, :].bitcast(I32))
+        def load_scale_rows(plane, src):
+            for q in range(4):
+                nc.sync.dma_start(plane[32 * q : 32 * q + 4, :], src[0, 4 * q : 4 * q + 4, :].bitcast(I32))
 
         def load_w2(b, tag):
             raw = keep.tile([P, PACK, PASS], F32, name="w2_raw", tag=tag)
@@ -62,7 +62,7 @@ def tile_list_litter_canopy_contrast_kernel(
 
         tab_s = keep.tile([P, T // 4], I32, name="tab_s", tag="stage_b")
         nc.vector.memset(tab_s[:], 0)
-        w1_s_raw = keep.tile([P, H // 4], I32, name="w1_s_raw")
+        w1_s_raw = keep.tile([P, H // 4], I32, name="w1_s_raw", tag="v_w1", align_bytes=64)
         nc.gpsimd.memset(w1_s_raw[:], 0)
 
         offs_t = load_list(offs, "offs_t")
@@ -73,28 +73,27 @@ def tile_list_litter_canopy_contrast_kernel(
         w2_raw = {0: load_w2(0, "stage_a")}
         w1_w_raw = keep.tile([P, H // 2], I32, name="w1_w_raw")
         nc.sync.dma_start(w1_w_raw[:], w1_words[0].bitcast(I32))
+        gain_t = keep.tile([P, PASSES, PACK], F32, name="gain_t")
+        nc.sync.dma_start(gain_t[:], gain.rearrange("(b p t) -> p b t", p=P, t=PACK))
+        load_scale_rows(tab_s, tab_scales)
         tab_w = keep.tile([P, T], I32, name="tab_w", tag="stage_c")
         nc.sync.dma_start(tab_w[:], tab_words[0].rearrange("p t i -> p (t i)").bitcast(I32))
-        load_scale_rows([nc.scalar] * 4, tab_s, tab_scales)
-        load_scale_rows([nc.scalar, nc.scalar, nc.gpsimd, nc.gpsimd], w1_s_raw, w1_scales)
-        gain_t = keep.tile([P, PASSES, PACK], F32, name="gain_t")
-        nc.gpsimd.dma_start(gain_t[:], gain.rearrange("(b p t) -> p b t", p=P, t=PACK))
+        load_scale_rows(w1_s_raw, w1_scales)
         slope_t = keep.tile([P, PASSES, PACK], F32, name="slope_t")
-        nc.gpsimd.dma_start(slope_t[:], slope.rearrange("(b p t) -> p b t", p=P, t=PACK))
+        nc.sync.dma_start(slope_t[:], slope.rearrange("(b p t) -> p b t", p=P, t=PACK))
         slope_f = slope_t[:].rearrange("p b t -> p (b t)")
 
-        w1_w = keep.tile([P, H], U16, name="w1_w", align_bytes=64)
-        nc.vector.tensor_copy(
-            w1_w[:].rearrange("p (b t m) -> p b t m", b=PASSES, t=PACK),
-            w1_w_raw[:].bitcast(U16).rearrange("p (b m t) -> p b t m", b=PASSES, t=PACK),
-        )
+        def deal(raw, dtype, b, name):
+            dealt = keep.tile([P, PASS], dtype, name=name, align_bytes=64)
+            nc.vector.tensor_copy(
+                dealt[:].rearrange("p (t m) -> p t m", t=PACK),
+                raw[:].bitcast(dtype)[:, PASS * b : PASS * (b + 1)].rearrange("p (m t) -> p t m", t=PACK),
+            )
+            return dealt
+
+        w1_w = [deal(w1_w_raw, U16, b, "w1_w%d" % b) for b in range(PASSES)]
         v_s = keep.tile([P, S], U8, name="v_s", align_bytes=64)
         nc.vector.tensor_copy(v_s[:], tab_s[:].bitcast(U8).indirect(offs_t[:]))
-        w1_s = keep.tile([P, H], U8, name="w1_s", align_bytes=64)
-        nc.vector.tensor_copy(
-            w1_s[:].rearrange("p (b t m) -> p b t m", b=PASSES, t=PACK),
-            w1_s_raw[:].bitcast(U8).rearrange("p (b m t) -> p b t m", b=PASSES, t=PACK),
-        )
         gabs = keep.tile([P, SLICES], F32, name="gabs")
         gflat = gain_t[:].rearrange("p b t -> p (b t)")
         nc.vector.scalar_tensor_tensor(gabs[:], gflat, -1.0, gflat, ALU.mult, ALU.max)
@@ -107,8 +106,8 @@ def tile_list_litter_canopy_contrast_kernel(
 
         def interleave(dst, src, copy=nc.scalar.copy):
             copy(
-                dst.rearrange("p (c i t) -> p c t i", i=4, t=PACK),
-                src.rearrange("p t (c i) -> p c t i", i=4),
+                dst.rearrange("p (c i t) -> p c t i", i=2, t=PACK),
+                src.rearrange("p t (c i) -> p c t i", i=2),
             )
 
         w2_bf, w2_q = {}, {}
@@ -118,10 +117,11 @@ def tile_list_litter_canopy_contrast_kernel(
         def round_w2(b, u):
             if u == 0:
                 w2_bf[b] = ring2.tile([P, PASS * PACK], BF16, name="w2_bf", align_bytes=64)
-            ms = slice(32 * u, 32 * (u + 1))
+            pair, half = divmod(u, 2)
+            ms = slice(64 * half, 64 * (half + 1))
             nc.scalar.copy(
-                w2_bf[b][:].rearrange("p (t m j) -> p m j t", t=PACK, j=PACK)[:, ms],
-                w2_raw[b][:].rearrange("p j (m t) -> p m j t", t=PACK)[:, ms],
+                w2_bf[b][:].rearrange("p (g e m j) -> p g m j e", g=2, e=2, j=PACK)[:, pair, ms],
+                w2_raw[b][:].rearrange("p j (m g e) -> p g m j e", g=2, e=2)[:, pair, ms],
             )
             if u == 3:
                 w2_q[b] = quantize(w2_bf[b], PASS, "w2q%d" % b)
@@ -135,7 +135,7 @@ def tile_list_litter_canopy_contrast_kernel(
             if o == 0:
                 w3_bf[b, u] = ring2.tile([P, W3_QUANT * PACK], BF16, name="w3_bf", align_bytes=64)
             interleave(w3_bf[b, u][:, o * PACK : (o + PIECE) * PACK], w3_raw[b][:, :, r * PIECE : (r + 1) * PIECE])
-            if o + PIECE == W3_QUANT:
+            if o + PIECE == W3_QUANT and (b, u) != (PASSES - 1, 1):
                 w3_q[b, u] = quantize(w3_bf[b, u], W3_QUANT, "w3q%d_%d" % (b, u))
 
         def round_x(b, u):
@@ -157,17 +157,19 @@ def tile_list_litter_canopy_contrast_kernel(
             cols = BANK // 16
             nc.vector.tensor_copy(t[:], tab_w[:].bitcast(U32).indirect(offs_t[:, hf * cols : (hf + 1) * cols]))
             v_w.append(t)
+            if hf == 0:
+                w1_s = [deal(w1_s_raw, U8, b, "w1_s%d" % b) for b in range(PASSES)]
         w3_raw[0] = load_w3(0, "stage_c")
 
         def first_stage(s, hf):
             b, t = divmod(s, PACK)
             tok = slice(hf * BANK, (hf + 1) * BANK)
-            rows = slice(s * P, (s + 1) * P)
+            rows = slice(t * P, (t + 1) * P)
             d1 = psum.tile([P, BANK], F32, name="d1")
             nc.tensor.matmul_mx(
                 out=d1[:],
-                lhsT=w1_w[:, rows].bitcast(FP4X4),
-                lhsT_scale=w1_s[:, rows],
+                lhsT=w1_w[b][:, rows].bitcast(FP4X4),
+                lhsT_scale=w1_s[b][:, rows],
                 rhs=v_w[hf][:].bitcast(FP8X4),
                 rhs_scale=v_s[:, tok],
                 start=True,
@@ -260,10 +262,11 @@ def tile_list_litter_canopy_contrast_kernel(
         for u in range(2):
             interleave(xa[:, u * 512 : (u + 1) * 512], x4[last][:, :, u * P : (u + 1) * P])
         litter(SLICES - 1, HM, PM)
-        xz = keep.tile([P, HM * PACK], BF16, name="xz", align_bytes=64)
+        xz = keep.tile([P, HM * PACK], BF16, name="xz", tag="w3q2_1_c", align_bytes=64)
         interleave(xz[:], x4[last][:, :, HM:PM], nc.vector.tensor_copy)
         qa = quantize(xa, HM, "xqa")
         qz = quantize(xz, HM, "xqz")
+        w3_q[last, 1] = quantize(w3_bf[last, 1], W3_QUANT, "w3q2_1")
         for n in range(NSLICES):
             second_stage(n, last, qa, slice(0, HM), False)
             second_stage(n, last, qz, slice(HM, PM), True)

@@ -27,6 +27,7 @@ NSLICES = N // P
 PIECE = 128
 W3_QUANT = 384
 PIECES_A_STEP = 3
+FUSED_FROM = SLICES - 2
 
 
 def tile_list_litter_canopy_contrast_kernel(
@@ -47,8 +48,8 @@ def tile_list_litter_canopy_contrast_kernel(
             return t
 
         def load_scale_rows(plane, src):
-            for q in range(4):
-                nc.sync.dma_start(plane[32 * q : 32 * q + 4, :], src[0, 4 * q : 4 * q + 4, :].bitcast(I32))
+            for r in range(4):
+                nc.sync.dma_start(plane[r:P:32, :], src[0, r:16:4, :].bitcast(I32))
 
         def load_w2(b, tag):
             raw = keep.tile([P, PACK, PASS], F32, name="w2_raw", tag=tag)
@@ -106,13 +107,13 @@ def tile_list_litter_canopy_contrast_kernel(
 
         def interleave(dst, src, copy=nc.scalar.copy):
             copy(
-                dst.rearrange("p (c i t) -> p c t i", i=2, t=PACK),
-                src.rearrange("p t (c i) -> p c t i", i=2),
+                dst.rearrange("p (c i t) -> p c t i", i=4, t=PACK),
+                src.rearrange("p t (c i) -> p c t i", i=4),
             )
 
         w2_bf, w2_q = {}, {}
         w3_raw, w3_bf, w3_q = {}, {}, {}
-        h_t, c_t, bent, x4, x_bf, x_q = {}, {}, {}, {}, {}, {}
+        h_t, c_t, l_t, bent, x4, x_bf, x_q = {}, {}, {}, {}, {}, {}, {}
 
         def round_w2(b, u):
             if u == 0:
@@ -161,40 +162,49 @@ def tile_list_litter_canopy_contrast_kernel(
                 w1_s = [deal(w1_s_raw, U8, b, "w1_s%d" % b) for b in range(PASSES)]
         w3_raw[0] = load_w3(0, "stage_c")
 
-        def first_stage(s, hf):
+        def first_stage(s):
             b, t = divmod(s, PACK)
-            tok = slice(hf * BANK, (hf + 1) * BANK)
             rows = slice(t * P, (t + 1) * P)
-            d1 = psum.tile([P, BANK], F32, name="d1")
-            nc.tensor.matmul_mx(
-                out=d1[:],
-                lhsT=w1_w[b][:, rows].bitcast(FP4X4),
-                lhsT_scale=w1_s[b][:, rows],
-                rhs=v_w[hf][:].bitcast(FP8X4),
-                rhs_scale=v_s[:, tok],
-                start=True,
-                stop=True,
-            )
-            d2 = psum.tile([P, BANK], F32, name="d2")
             codes, scales = w2_q[b]
-            nc.tensor.matmul_mx(
-                out=d2[:],
-                lhsT=codes[:, t * P : (t + 1) * P].bitcast(FP8X4),
-                lhsT_scale=scales[:, t * P : (t + 1) * P],
-                rhs=v_w[hf][:].bitcast(FP8X4),
-                rhs_scale=v_s[:, tok],
-                start=True,
-                stop=True,
-            )
-            a = ring4.tile([P, BANK], F32, name="a")
-            nc.scalar.activation(a[:], d1[:], ACT.Copy, scale=gabs[:, s : s + 1])
-            if hf == 0:
-                h_t[s] = ring4.tile([P, S], F32, name="h")
-            nc.vector.scalar_tensor_tensor(h_t[s][:, tok], d2[:], gabs[:, s : s + 1], a[:], ALU.mult, ALU.max)
+            h_t[s] = ring4.tile([P, S], F32, name="h")
+            scaled = []
+            for hf in range(HALVES):
+                d1 = psum.tile([P, BANK], F32, name="d1")
+                nc.tensor.matmul_mx(
+                    out=d1[:],
+                    lhsT=w1_w[b][:, rows].bitcast(FP4X4),
+                    lhsT_scale=w1_s[b][:, rows],
+                    rhs=v_w[hf][:].bitcast(FP8X4),
+                    rhs_scale=v_s[:, hf * BANK : (hf + 1) * BANK],
+                    start=True,
+                    stop=True,
+                )
+                a = ring4.tile([P, BANK], F32, name="a")
+                nc.scalar.activation(a[:], d1[:], ACT.Copy, scale=gabs[:, s : s + 1])
+                scaled.append(a)
+            for hf in range(HALVES):
+                tok = slice(hf * BANK, (hf + 1) * BANK)
+                d2 = psum.tile([P, BANK], F32, name="d2")
+                nc.tensor.matmul_mx(
+                    out=d2[:],
+                    lhsT=codes[:, rows].bitcast(FP8X4),
+                    lhsT_scale=scales[:, rows],
+                    rhs=v_w[hf][:].bitcast(FP8X4),
+                    rhs_scale=v_s[:, tok],
+                    start=True,
+                    stop=True,
+                )
+                nc.vector.scalar_tensor_tensor(
+                    h_t[s][:, tok], d2[:], gabs[:, s : s + 1], scaled[hf][:], ALU.mult, ALU.max
+                )
 
-        def canopy(s):
+        def pick_canopy(s):
             c_t[s] = keep.tile([P, PM], F32, name="c")
             nc.vector.tensor_copy(c_t[s][:], h_t[s][:].indirect(pos2_t[:]))
+
+        def pick_litter(s):
+            l_t[s] = ring2.tile([P, PM], F32, name="l")
+            nc.vector.tensor_copy(l_t[s][:], h_t[s][:].indirect(pos1_t[:]))
 
         def bend(s):
             bent[s] = ring2.tile([P, PM], F32, name="bent")
@@ -204,9 +214,12 @@ def tile_list_litter_canopy_contrast_kernel(
             b, t = divmod(s, PACK)
             if t == 0:
                 x4[b] = ring2.tile([P, PACK, PM], F32, name="x4")
-            nc.vector.tensor_tensor(
-                x4[b][:, t, lo:hi], h_t[s][:].indirect(pos1_t[:, lo // 16 : hi // 16]), bent[s][:, lo:hi], ALU.mult
-            )
+            if s < FUSED_FROM:
+                nc.gpsimd.tensor_tensor(x4[b][:, t, :], l_t[s][:], bent[s][:], ALU.mult)
+            else:
+                nc.vector.tensor_tensor(
+                    x4[b][:, t, lo:hi], h_t[s][:].indirect(pos1_t[:, lo // 16 : hi // 16]), bent[s][:, lo:hi], ALU.mult
+                )
 
         y_ps = {}
 
@@ -232,31 +245,33 @@ def tile_list_litter_canopy_contrast_kernel(
         jobs = jobs + [(round_w3, b, r) for b in range(PASSES) for r in range(NSLICES)]
         for s in range(SLICES + 1):
             if s < SLICES:
-                first_stage(s, 0)
+                first_stage(s)
             if s >= 2:
                 bend(s - 2)
             if s >= 1:
-                canopy(s - 1)
-            if s < SLICES:
-                first_stage(s, 1)
+                pick_canopy(s - 1)
+            if s >= 2:
+                litter(s - 2)
+            if s < FUSED_FROM:
+                pick_litter(s)
             if s >= 1:
-                count = PIECES_A_STEP - 1 if s in (9, 11) else PIECES_A_STEP
+                count = 1 if s == SLICES else PIECES_A_STEP - 1 if s in (9, 11) else PIECES_A_STEP
                 for fn, b, u in jobs[:count]:
                     fn(b, u)
                 jobs = jobs[count:]
             if s >= 2:
-                litter(s - 2)
                 if (s - 2) % PACK == PACK - 1:
                     jobs = [(round_x, (s - 2) // PACK, u) for u in range(4)] + jobs
             if s == SLICES - 1:
                 for b in range(PASSES - 1):
                     for n in range(4, NSLICES):
                         second_stage(n, b, x_q[b], slice(0, PM), False)
-        assert not jobs
 
         last = PASSES - 1
         HM = PM // 2
         bend(SLICES - 1)
+        for fn, b, u in jobs:
+            fn(b, u)
         litter(SLICES - 1, 0, HM)
         xa = keep.tile([P, HM * PACK], BF16, name="xa", align_bytes=64)
         for u in range(2):

from contextlib import ExitStack

import concourse.mybir as mybir

K, H, N, T, S, PM, PJ = 512, 1536, 768, 4096, 1024, 512, 256
FLOPS = 2 * (2 * K * H * S + H * N * PM)

F32 = mybir.dt.float32
BF16 = mybir.dt.bfloat16
I32 = mybir.dt.int32
U32 = mybir.dt.uint32
U16 = mybir.dt.uint16
U8 = mybir.dt.uint8
FP8X4 = mybir.dt.float8_e4m3fn_x4
FP4X4 = mybir.dt.float4_e2m1fn_x4
ALU = mybir.AluOpType
ACT = mybir.ActivationFunctionType

P = 128
PACK = 4
PASS = P * PACK
BANK = 512
PASSES = H // PASS
SLICES = H // P
HALVES = S // BANK
NSLICES = N // P
PIECE = 128
W3_QUANT = 384
PIECES_A_STEP = 3
FUSED_FROM = SLICES - 2


def tile_list_litter_canopy_contrast_kernel(
    tc, tab_words, tab_scales, offs, pos1, pos2, pos3, pos4, w1_words, w1_scales, w2, gain, slope, w3, out
):
    nc = tc.nc
    with ExitStack() as ctx:
        keep = ctx.enter_context(tc.tile_pool(name="keep", bufs=1))
        ring2 = ctx.enter_context(tc.tile_pool(name="ring2", bufs=2))
        ring3 = ctx.enter_context(tc.tile_pool(name="ring3", bufs=3))
        ring4 = ctx.enter_context(tc.tile_pool(name="ring4", bufs=4))
        psum = ctx.enter_context(tc.psum_pool(name="psum", bufs=2))
        psum_y = ctx.enter_context(tc.psum_pool(name="psum_y", bufs=4))

        def load_list(src, name):
            t = keep.tile(list(src.shape), U16, name=name)
            nc.sync.dma_start(t[:], src)
            return t

        def load_scale_rows(plane, src):
            for r in range(4):
                nc.sync.dma_start(plane[r:P:32, :], src[0, r:16:4, :].bitcast(I32))

        def load_w2(b, tag):
            raw = keep.tile([P, PACK, PASS], F32, name="w2_raw", tag=tag)
            nc.sync.dma_start(raw[:], w2[:, PASS * b : PASS * (b + 1)].rearrange("(p j) c -> p j c", j=PACK))
            return raw

        def load_w3(b, tag):
            raw = keep.tile([P, PACK, N], F32, name="w3_raw", tag=tag)
            nc.sync.dma_start(raw[:], w3[PASS * b : PASS * (b + 1), :].rearrange("(p j) n -> p j n", j=PACK))
            return raw

        tab_s = keep.tile([P, T // 4], I32, name="tab_s", tag="stage_b")
        nc.vector.memset(tab_s[:], 0)
        w1_s_raw = keep.tile([P, H // 4], I32, name="w1_s_raw", tag="v_w1", align_bytes=64)
        nc.gpsimd.memset(w1_s_raw[:], 0)

        offs_t = load_list(offs, "offs_t")
        pos2_t = load_list(pos2, "pos2_t")
        pos1_t = load_list(pos1, "pos1_t")
        pos3_t = load_list(pos3, "pos3_t")
        pos4_t = load_list(pos4, "pos4_t")
        w2_raw = {0: load_w2(0, "stage_a")}
        w1_w_raw = keep.tile([P, H // 2], I32, name="w1_w_raw")
        nc.sync.dma_start(w1_w_raw[:], w1_words[0].bitcast(I32))
        gain_t = keep.tile([P, PASSES, PACK], F32, name="gain_t")
        nc.sync.dma_start(gain_t[:], gain.rearrange("(b p t) -> p b t", p=P, t=PACK))
        load_scale_rows(tab_s, tab_scales)
        tab_w = keep.tile([P, T], I32, name="tab_w", tag="stage_c")
        nc.sync.dma_start(tab_w[:], tab_words[0].rearrange("p t i -> p (t i)").bitcast(I32))
        load_scale_rows(w1_s_raw, w1_scales)
        slope_t = keep.tile([P, PASSES, PACK], F32, name="slope_t")
        nc.sync.dma_start(slope_t[:], slope.rearrange("(b p t) -> p b t", p=P, t=PACK))
        slope_f = slope_t[:].rearrange("p b t -> p (b t)")

        def deal(raw, dtype, b, name):
            dealt = keep.tile([P, PASS], dtype, name=name, align_bytes=64)
            nc.vector.tensor_copy(
                dealt[:].rearrange("p (t m) -> p t m", t=PACK),
                raw[:].bitcast(dtype)[:, PASS * b : PASS * (b + 1)].rearrange("p (m t) -> p t m", t=PACK),
            )
            return dealt

        w1_w = [deal(w1_w_raw, U16, b, "w1_w%d" % b) for b in range(PASSES)]
        v_s = keep.tile([P, S], U8, name="v_s", align_bytes=64)
        nc.vector.tensor_copy(v_s[:], tab_s[:].bitcast(U8).indirect(offs_t[:]))
        gabs = keep.tile([P, SLICES], F32, name="gabs")
        gflat = gain_t[:].rearrange("p b t -> p (b t)")
        nc.vector.scalar_tensor_tensor(gabs[:], gflat, -1.0, gflat, ALU.mult, ALU.max)

        def quantize(grouped, width, name):
            codes = keep.tile([P, width], U32, name=name + "_c", align_bytes=64)
            scales = keep.tile([P, width], U8, name=name + "_s", align_bytes=64)
            nc.vector.quantize_mx(out=codes[:].bitcast(FP8X4), scales=scales[:], in_=grouped[:])
            return codes, scales

        def interleave(dst, src, copy=nc.scalar.copy):
            copy(
                dst.rearrange("p (c i t) -> p c t i", i=4, t=PACK),
                src.rearrange("p t (c i) -> p c t i", i=4),
            )

        w2_bf, w2_q = {}, {}
        w3_raw, w3_bf, w3_q = {}, {}, {}
        h_t, c_t, l_t, bent, x4, x_bf, x_q = {}, {}, {}, {}, {}, {}, {}

        def round_w2(b, u):
            if u == 0:
                w2_bf[b] = ring2.tile([P, PASS * PACK], BF16, name="w2_bf", align_bytes=64)
            pair, half = divmod(u, 2)
            ms = slice(64 * half, 64 * (half + 1))
            nc.scalar.copy(
                w2_bf[b][:].rearrange("p (g e m j) -> p g m j e", g=2, e=2, j=PACK)[:, pair, ms],
                w2_raw[b][:].rearrange("p j (m g e) -> p g m j e", g=2, e=2)[:, pair, ms],
            )
            if u == 3:
                w2_q[b] = quantize(w2_bf[b], PASS, "w2q%d" % b)
                if b == 0:
                    w2_raw[1] = load_w2(1, "stage_a")
                else:
                    w3_raw[b] = load_w3(b, "stage_a" if b == 1 else "stage_b")

        def round_w3(b, r):
            u, o = divmod(r * PIECE, W3_QUANT)
            if o == 0:
                w3_bf[b, u] = ring2.tile([P, W3_QUANT * PACK], BF16, name="w3_bf", align_bytes=64)
            interleave(w3_bf[b, u][:, o * PACK : (o + PIECE) * PACK], w3_raw[b][:, :, r * PIECE : (r + 1) * PIECE])
            if o + PIECE == W3_QUANT and (b, u) != (PASSES - 1, 1):
                w3_q[b, u] = quantize(w3_bf[b, u], W3_QUANT, "w3q%d_%d" % (b, u))

        def round_x(b, u):
            if u == 0:
                x_bf[b] = ring2.tile([P, PM * PACK], BF16, name="x_bf", align_bytes=64)
            interleave(x_bf[b][:, u * PIECE * PACK : (u + 1) * PIECE * PACK], x4[b][:, :, u * PIECE : (u + 1) * PIECE])
            if u == 3:
                x_q[b] = quantize(x_bf[b], PM, "xq%d" % b)
                for n in range(4):
                    second_stage(n, b, x_q[b], slice(0, PM), False)

        for u in range(4):
            round_w2(0, u)
        w2_raw[2] = load_w2(2, "stage_b")

        v_w = []
        for hf in range(HALVES):
            t = keep.tile([P, BANK], U32, name="v_w%d" % hf, align_bytes=64)
            cols = BANK // 16
            nc.vector.tensor_copy(t[:], tab_w[:].bitcast(U32).indirect(offs_t[:, hf * cols : (hf + 1) * cols]))
            v_w.append(t)
            if hf == 0:
                w1_s = [deal(w1_s_raw, U8, b, "w1_s%d" % b) for b in range(PASSES)]
        w3_raw[0] = load_w3(0, "stage_c")

        def first_stage(s):
            b, t = divmod(s, PACK)
            rows = slice(t * P, (t + 1) * P)
            codes, scales = w2_q[b]
            h_t[s] = ring4.tile([P, S], F32, name="h")
            scaled = []
            for hf in range(HALVES):
                d1 = psum.tile([P, BANK], F32, name="d1")
                nc.tensor.matmul_mx(
                    out=d1[:],
                    lhsT=w1_w[b][:, rows].bitcast(FP4X4),
                    lhsT_scale=w1_s[b][:, rows],
                    rhs=v_w[hf][:].bitcast(FP8X4),
                    rhs_scale=v_s[:, hf * BANK : (hf + 1) * BANK],
                    start=True,
                    stop=True,
                )
                a = ring4.tile([P, BANK], F32, name="a")
                nc.scalar.activation(a[:], d1[:], ACT.Copy, scale=gabs[:, s : s + 1])
                scaled.append(a)
            for hf in range(HALVES):
                tok = slice(hf * BANK, (hf + 1) * BANK)
                d2 = psum.tile([P, BANK], F32, name="d2")
                nc.tensor.matmul_mx(
                    out=d2[:],
                    lhsT=codes[:, rows].bitcast(FP8X4),
                    lhsT_scale=scales[:, rows],
                    rhs=v_w[hf][:].bitcast(FP8X4),
                    rhs_scale=v_s[:, tok],
                    start=True,
                    stop=True,
                )
                nc.vector.scalar_tensor_tensor(
                    h_t[s][:, tok], d2[:], gabs[:, s : s + 1], scaled[hf][:], ALU.mult, ALU.max
                )

        def pick_canopy(s):
            c_t[s] = keep.tile([P, PM], F32, name="c")
            nc.vector.tensor_copy(c_t[s][:], h_t[s][:].indirect(pos2_t[:]))

        def pick_litter(s):
            l_t[s] = ring2.tile([P, PM], F32, name="l")
            nc.vector.tensor_copy(l_t[s][:], h_t[s][:].indirect(pos1_t[:]))

        def bend(s):
            bent[s] = ring2.tile([P, PM], F32, name="bent")
            nc.scalar.activation(bent[s][:], c_t[s][:], ACT.Tanh, scale=slope_f[:, s : s + 1])

        def litter(s, lo=0, hi=PM):
            b, t = divmod(s, PACK)
            if t == 0:
                x4[b] = ring2.tile([P, PACK, PM], F32, name="x4")
            if s < FUSED_FROM:
                nc.gpsimd.tensor_tensor(x4[b][:, t, :], l_t[s][:], bent[s][:], ALU.mult)
            else:
                nc.vector.tensor_tensor(
                    x4[b][:, t, lo:hi], h_t[s][:].indirect(pos1_t[:, lo // 16 : hi // 16]), bent[s][:, lo:hi], ALU.mult
                )

        y_ps = {}

        def second_stage(n, b, xq, cols, stop):
            if b == 0:
                if n < 4:
                    y_ps[n] = psum_y.tile([P, PM], F32, name="y")
                else:
                    y_ps[n] = psum.tile([P, PM], F32, name="d1" if n == 4 else "d2")
            u, o = divmod(n * P, W3_QUANT)
            codes, scales = w3_q[b, u]
            nc.tensor.matmul_mx(
                out=y_ps[n][:, cols],
                lhsT=codes[:, o : o + P].bitcast(FP8X4),
                lhsT_scale=scales[:, o : o + P],
                rhs=xq[0][:].bitcast(FP8X4),
                rhs_scale=xq[1][:],
                start=(b == 0),
                stop=stop,
            )

        jobs = [(round_w2, b, u) for b in range(1, PASSES) for u in range(4)]
        jobs = jobs + [(round_w3, b, r) for b in range(PASSES) for r in range(NSLICES)]
        for s in range(SLICES + 1):
            if s < SLICES:
                first_stage(s)
            if s >= 2:
                bend(s - 2)
            if s >= 1:
                pick_canopy(s - 1)
            if s >= 2:
                litter(s - 2)
            if s < FUSED_FROM:
                pick_litter(s)
            if s >= 1:
                count = 1 if s == SLICES else PIECES_A_STEP - 1 if s in (9, 11) else PIECES_A_STEP
                for fn, b, u in jobs[:count]:
                    fn(b, u)
                jobs = jobs[count:]
            if s >= 2:
                if (s - 2) % PACK == PACK - 1:
                    jobs = [(round_x, (s - 2) // PACK, u) for u in range(4)] + jobs
            if s == SLICES - 1:
                for b in range(PASSES - 1):
                    for n in range(4, NSLICES):
                        second_stage(n, b, x_q[b], slice(0, PM), False)

        last = PASSES - 1
        HM = PM // 2
        bend(SLICES - 1)
        for fn, b, u in jobs:
            fn(b, u)
        litter(SLICES - 1, 0, HM)
        xa = keep.tile([P, HM * PACK], BF16, name="xa", align_bytes=64)
        for u in range(2):
            interleave(xa[:, u * 512 : (u + 1) * 512], x4[last][:, :, u * P : (u + 1) * P])
        litter(SLICES - 1, HM, PM)
        xz = keep.tile([P, HM * PACK], BF16, name="xz", tag="w3q2_1_c", align_bytes=64)
        interleave(xz[:], x4[last][:, :, HM:PM], nc.vector.tensor_copy)
        qa = quantize(xa, HM, "xqa")
        qz = quantize(xz, HM, "xqz")
        w3_q[last, 1] = quantize(w3_bf[last, 1], W3_QUANT, "w3q2_1")
        for n in range(NSLICES):
            second_stage(n, last, qa, slice(0, HM), False)
            second_stage(n, last, qz, slice(HM, PM), True)

        freed = ["w3q2_0_c", "w3q2_1_c", "xqa_c", "xqz_c", "diff4", "diff5"]
        y_sb = {}
        near = {}
        for n in range(NSLICES + 1):
            if n < NSLICES:
                y_sb[n] = keep.tile([P, PM], F32, name="y_sb%d" % n)
                nc.scalar.copy(y_sb[n][:], y_ps[n][:])
                near[n] = keep.tile([P, PJ], F32, name="near%d" % n)
                nc.vector.tensor_copy(near[n][:], y_sb[n][:].indirect(pos3_t[:]))
            if n >= 1:
                diff = keep.tile([P, PJ], F32, name="diff", tag=freed[n - 1], align_bytes=64)
                nc.vector.tensor_tensor(diff[:], y_sb[n - 1][:].indirect(pos4_t[:]), near[n - 1][:], ALU.subtract)
                res = keep.tile([P, PJ], F32, name="res%d" % n)
                nc.scalar.activation(res[:], diff[:], ACT.Abs)
                nc.sync.dma_start(out[(n - 1) * P : n * P, :], res[:])
